import numpy as np
import ml_dtypes


def mxq(x, axis, fmt="e4m3"):
    dtype, down = {"e4m3": (ml_dtypes.float8_e4m3fn, 7), "e5m2": (ml_dtypes.float8_e5m2, 14)}[fmt]
    v = np.moveaxis(np.asarray(x, np.float32).astype(ml_dtypes.bfloat16).astype(np.float64), axis, -1)
    blocks = v.reshape(v.shape[:-1] + (-1, 32))
    amax = np.abs(blocks).max(-1, keepdims=True)
    byte = np.maximum(np.where(amax > 0, np.frexp(amax)[1] - 1 + 127, 0) - down, 1)
    scale = np.exp2(byte - 127.0)
    codes = (blocks / scale).astype(np.float32).astype(dtype).astype(np.float64)
    return np.moveaxis((codes * scale).reshape(v.shape), -1, axis)


WIDE = False


def mx_kscale(k):
    if not WIDE:
        return np.ones(k)
    levels = np.array([30, -30])
    if k % 512:
        return np.exp2(np.random.permutation(np.resize(levels, k // 32))).repeat(32)
    a = np.empty((k // 512, 16))
    for p in range(k // 512):
        a[p, :8] = np.random.permutation(np.resize(levels, 8))
        for g in range(8):
            far = levels[np.abs(levels - a[p, g]) >= 10]
            a[p, g + 8] = far[np.random.randint(len(far))]
    return np.exp2(a.ravel()).repeat(32)


def f64(x):
    return np.asarray(x).astype(np.float64)


E2M1 = np.array([0.0, 0.5, 1.0, 1.5, 2.0, 3.0, 4.0, 6.0, -0.0, -0.5, -1.0, -1.5, -2.0, -3.0, -4.0, -6.0])


def pack_weight(w, fmt):
    k, n = w.shape
    w = f64(np.asarray(w, np.float32).astype(ml_dtypes.bfloat16)).reshape(k // 32, 32, n)
    amax = np.abs(w).max(1)
    if fmt == "e4m3":
        byte = np.frexp(amax)[1] - 1 + 127 - 7
    else:
        mant, ex = np.frexp(amax / 6.0)
        byte = np.where(mant > 0.5, ex, ex - 1) + 127
    byte = np.clip(np.where(amax > 0, byte, 1), 1, 254)
    scaled = (w * np.exp2(127.0 - byte)[:, None, :]).reshape(k, n).astype(np.float32)
    by_word = np.ascontiguousarray(scaled.reshape(k // 512, 128, 4, n).transpose(0, 1, 3, 2))
    if fmt == "e4m3":
        words = by_word.astype(ml_dtypes.float8_e4m3fn).view(np.uint8)
    else:
        c = by_word.astype(ml_dtypes.float4_e2m1fn).view(np.uint8) & 0xF
        words = (c[..., 0::2] | (c[..., 1::2] << 4)).reshape(k // 512, 128, 2 * n)
    return np.ascontiguousarray(words), np.ascontiguousarray(byte.astype(np.uint8).reshape(k // 512, 16, n))


def unpack_weight(words, scales, fmt):
    g, _, n = scales.shape
    words = np.ascontiguousarray(words).reshape(g, 128, n, -1)
    if fmt == "e4m3":
        vals = words.view(ml_dtypes.float8_e4m3fn).astype(np.float64)
    else:
        nib = np.empty((g, 128, n, 4), np.uint8)
        nib[..., 0::2] = words & 0xF
        nib[..., 1::2] = words >> 4
        vals = E2M1[nib]
    vals = vals * np.repeat(np.exp2(scales.astype(np.float64) - 127.0), 8, axis=1)[..., None]
    return vals.transpose(0, 1, 3, 2).reshape(g * 512, n)


def silu(v):
    return v / (1.0 + np.exp(-np.maximum(v, -700.0)))


K, L, R, M, T = 1536, 1024, 512, 1024, 512


def setup_inputs():
    n = np.random.standard_normal
    s1 = mx_kscale(K)[:, None]
    s2 = mx_kscale(L)[:, None]
    u = mx_kscale(R)[:, None]
    p_w = pack_weight(n((R, M)) / np.sqrt(R) / u, "e2m1")
    return {
        "x": (n((K, T)) * s1).astype(np.float32),
        "wx": (n((K, R)) / np.sqrt(K) / s1 * u.T).astype(np.float32),
        "c": (n((L, T)) * s2).astype(np.float32),
        "wc": (n((L, R)) / np.sqrt(L) / s2).astype(np.float32),
        "w_words": p_w[0],
        "w_scales": p_w[1],
        "b": (0.3 * n(1024)).astype(np.float32),
    }


def reference(x, wx, c, wc, w_words, w_scales, b):
    x_ = mxq(f64(x), 0, "e4m3")
    wx_ = mxq(f64(wx), 0, "e4m3")
    c_ = mxq(f64(c), 0, "e5m2")
    wc_ = mxq(f64(wc), 0, "e4m3")
    w_ = unpack_weight(w_words, w_scales, "e2m1")
    h_ = mxq((wx_.T @ x_) * (wc_.T @ c_), 0, "e4m3")
    y = h_.T @ w_
    return silu(y + f64(b)[None, :])

@@ -1,0 +1,304 @@
+from contextlib import ExitStack
+
+import concourse.mybir as mybir
+from concourse.masks import make_identity
+
+K, L, R, M, T = 1536, 1024, 512, 1024, 512
+FLOPS = 2 * (K * R * T + L * R * T + R * M * T)
+
+F32 = mybir.dt.float32
+BF16 = mybir.dt.bfloat16
+I32 = mybir.dt.int32
+U32 = mybir.dt.uint32
+U8 = mybir.dt.uint8
+E4M3 = mybir.dt.float8_e4m3fn_x4
+E5M2 = mybir.dt.float8_e5m2_x4
+E2M1 = mybir.dt.float4_e2m1fn_x4
+SILU = mybir.ActivationFunctionType.Silu
+
+P = 128
+PACK = 4
+K_PASS = P * PACK
+BANK = 512
+TOK = 128
+HALF = 256
+
+
+def tile_mix_bilin_tm_silu_kernel(tc, x, wx, c, wc, w_words, w_scales, b, out):
+    nc = tc.nc
+    x_passes = K // K_PASS
+    c_passes = L // K_PASS
+    tiles = T // TOK
+
+    with ExitStack() as ctx:
+        sb = ctx.enter_context(tc.tile_pool(name="sb", bufs=1))
+        ps = ctx.enter_context(tc.psum_pool(name="ps", bufs=1))
+        ctx.enter_context(tc.manual_schedule())
+
+        def copy_on(engine, dst, src):
+            if engine == "vector":
+                nc.vector.tensor_copy(out=dst, in_=src)
+            else:
+                nc.scalar.copy(out=dst, in_=src)
+
+        def load_rows(name, rows):
+            raw = sb.tile([P, PACK, rows.shape[1]], F32, name=name)
+            nc.sync.dma_start(out=raw[:], in_=rows.rearrange("(p j) w -> p j w", j=PACK))
+            return raw
+
+        def operand(name, width):
+            codes = sb.tile([P, width], U32, name=name + "_codes", align_bytes=64)
+            scales = sb.tile([P, width], U8, name=name + "_scales", align_bytes=64)
+            return codes, scales
+
+        def round_columns(engine, name, raw, first, count):
+            grouped = sb.tile([P, count * PACK], BF16, name=name, align_bytes=64)
+            copy_on(
+                engine,
+                grouped[:].rearrange("p (q i j) -> p q j i", i=4, j=PACK),
+                raw[:, :, first : first + count].rearrange("p j (q i) -> p q j i", i=4),
+            )
+            return grouped
+
+        def round_weight_half(engine, name, raw, half):
+            grouped = sb.tile([P, HALF * PACK], BF16, name=name, align_bytes=64)
+            copy_on(
+                engine,
+                grouped[:].rearrange("p (s m j) -> p m j s", s=2, j=PACK),
+                raw[:].rearrange("p j (m s) -> p m j s", s=PACK)[:, :, :, 2 * half : 2 * half + 2],
+            )
+            return grouped
+
+        def quantize(op, first, grouped, fmt):
+            count = grouped.shape[1] // PACK
+            nc.vector.quantize_mx(
+                out=op[0][:, first : first + count].bitcast(fmt),
+                scales=op[1][:, first : first + count],
+                in_=grouped[:],
+            )
+
+        def pass_rows(g):
+            return slice(g * K_PASS, (g + 1) * K_PASS)
+
+        def tokens(i):
+            return slice(i * TOK, (i + 1) * TOK)
+
+        w_plane = sb.tile([P, M], U8, name="w_plane", align_bytes=64)
+        nc.vector.memset(w_plane[:].bitcast(I32), 0)
+        ident = sb.tile([P, P], F32, name="ident")
+        make_identity(nc, ident[:])
+        warm = sb.tile([P, 1], F32, name="warm")
+        nc.scalar.activation(out=warm[:], in_=ident[:, 0:1], func=SILU)
+
+        wc_raw, c_raw, wx_raw, x_raw = {}, {}, {}, {}
+        wc_raw[0] = load_rows("wc_raw0", wc[pass_rows(0), :])
+        b_cols = sb.tile([P, M // P], F32, name="b_cols")
+        nc.sync.dma_start(out=b_cols[:], in_=b.rearrange("(n m) -> n m", n=P))
+        for q in range(4):
+            nc.sync.dma_start(
+                out=w_plane[32 * q : 32 * q + 4, :].bitcast(I32),
+                in_=w_scales[0, 4 * q : 4 * q + 4, :].bitcast(I32),
+            )
+        c_raw[0] = load_rows("c_raw0", c[pass_rows(0), :])
+        wc_raw[1] = load_rows("wc_raw1", wc[pass_rows(1), :])
+        c_raw[1] = load_rows("c_raw1", c[pass_rows(1), :])
+
+        def load_x(i, g):
+            x_raw[i, g] = load_rows("x_raw%d_%d" % (i, g), x[pass_rows(g), tokens(i)])
+
+        wx_raw[0] = load_rows("wx_raw0", wx[pass_rows(0), :])
+        wx_raw[1] = load_rows("wx_raw1", wx[pass_rows(1), :])
+        load_x(0, 0)
+        load_x(0, 1)
+        wx_raw[2] = load_rows("wx_raw2", wx[pass_rows(2), :])
+        load_x(0, 2)
+        w_codes = sb.tile([P, 2 * M], U8, name="w_codes", align_bytes=64)
+        nc.sync.dma_start(out=w_codes[:].bitcast(I32), in_=w_words[0].bitcast(I32))
+        for i in range(1, tiles):
+            for g in range(x_passes):
+                load_x(i, g)
+
+        bias = sb.tile([P, M], F32, name="bias")
+        bias_ps = {}
+        for u in range(2):
+            bias_ps[u] = ps.tile([P, BANK], F32, name="bias_ps%d" % u, tag="px%d" % (2 + u))
+            for m in range(4):
+                col = 4 * u + m
+                nc.tensor.transpose(
+                    bias_ps[u][:, m * P : (m + 1) * P],
+                    b_cols[:, col : col + 1].to_broadcast([P, P]),
+                    ident[:],
+                )
+
+        def weight_pass(name, raw, engines):
+            op = operand(name, R)
+            halves = [round_weight_half(engines[u], "%s_bf%d" % (name, u), raw, u) for u in range(2)]
+            for u in range(2):
+                quantize(op, u * HALF, halves[u], E4M3)
+            return op
+
+        pc_ps = [ps.tile([P, BANK], F32, name="pc_ps%d" % s, tag="acc%d" % s) for s in range(PACK)]
+        for g in range(c_passes):
+            wc_op = weight_pass("wc%d" % g, wc_raw[g], ("vector", "scalar"))
+            if g == 0:
+                for u in range(2):
+                    nc.scalar.copy(
+                        out=bias[:].rearrange("p (n m) -> p n m", m=M // P)[:, :, 4 * u : 4 * u + 4],
+                        in_=bias_ps[u][:].rearrange("p (m n) -> p n m", m=4),
+                    )
+            c_op = operand("c%d" % g, T)
+            c_lo = round_columns("vector", "c_bf%d_0" % g, c_raw[g], 0, HALF)
+            c_hi = round_columns("scalar", "c_bf%d_1" % g, c_raw[g], HALF, HALF)
+            quantize(c_op, 0, c_lo, E5M2)
+            quantize(c_op, HALF, c_hi, E5M2)
+            for s in range(PACK):
+                nc.tensor.matmul_mx(
+                    out=pc_ps[s][:],
+                    lhsT=wc_op[0][:, s * P : (s + 1) * P].bitcast(E4M3),
+                    lhsT_scale=wc_op[1][:, s * P : (s + 1) * P],
+                    rhs=c_op[0][:].bitcast(E5M2),
+                    rhs_scale=c_op[1][:],
+                    start=(g == 0),
+                    stop=(g == c_passes - 1),
+                )
+
+        pc_rows = sb.tile([P, PACK, T], F32, name="pc_rows")
+        for s in range(PACK):
+            nc.scalar.copy(out=pc_rows[:, s, :], in_=pc_ps[s][:])
+        pc = {}
+
+        def interleave_pc(i):
+            pc[i] = sb.tile([P, TOK * PACK], F32, name="pc%d" % i)
+            nc.scalar.copy(
+                out=pc[i][:].rearrange("p (t s) -> p t s", s=PACK),
+                in_=pc_rows[:, :, tokens(i)].rearrange("p s t -> p t s"),
+            )
+
+        wx_op, x_bf, x_op, px_ps, h_bf, h_op, y_ps, z = {}, {}, {}, {}, {}, {}, {}, {}
+
+        def round_x(engine, i, g):
+            x_bf[i, g] = round_columns(engine, "x_bf%d_%d" % (i, g), x_raw[i, g], 0, TOK)
+
+        def quantize_x(i, g):
+            x_op[i, g] = operand("x%d_%d" % (i, g), TOK)
+            quantize(x_op[i, g], 0, x_bf[i, g], E4M3)
+
+        def project_x(i, g, slots):
+            if i not in px_ps:
+                px_ps[i] = ps.tile([P, BANK], F32, name="px_ps%d" % i, tag="px%d" % i)
+            for s in slots:
+                nc.tensor.matmul_mx(
+                    out=px_ps[i][:, s * TOK : (s + 1) * TOK],
+                    lhsT=wx_op[g][0][:, s * P : (s + 1) * P].bitcast(E4M3),
+                    lhsT_scale=wx_op[g][1][:, s * P : (s + 1) * P],
+                    rhs=x_op[i, g][0][:].bitcast(E4M3),
+                    rhs_scale=x_op[i, g][1][:],
+                    start=(g == 0 and s == 0),
+                    stop=(g == x_passes - 1 and s == PACK - 1),
+                )
+
+        def x_pass(i, g):
+            quantize_x(i, g)
+            project_x(i, g, range(PACK))
+
+        def multiply(i):
+            h_bf[i] = sb.tile([P, TOK * PACK], BF16, name="h_bf%d" % i, align_bytes=64)
+            nc.vector.tensor_mul(
+                out=h_bf[i][:].rearrange("p (t s) -> p t s", s=PACK),
+                in0=px_ps[i][:].rearrange("p (s t) -> p t s", s=PACK),
+                in1=pc[i][:].rearrange("p (t s) -> p t s", s=PACK),
+            )
+
+        def quantize_h(i):
+            h_op[i] = operand("h%d" % i, TOK)
+            quantize(h_op[i], 0, h_bf[i], E4M3)
+
+        def project_h(i, u):
+            y_ps[i, u] = ps.tile([P, BANK], F32, name="y_ps%d_%d" % (i, u), tag="acc%d" % ((2 * i + u) % 4))
+            nc.tensor.matmul_mx(
+                out=y_ps[i, u][:],
+                lhsT=h_op[i][0][:].bitcast(E4M3),
+                lhsT_scale=h_op[i][1][:],
+                rhs=w_codes[:, 2 * u * BANK : 2 * (u + 1) * BANK].bitcast(E2M1),
+                rhs_scale=w_plane[:, u * BANK : (u + 1) * BANK],
+                start=True,
+                stop=True,
+            )
+
+        def add_bias(i, u):
+            z[i, u] = sb.tile([P, BANK], F32, name="z%d_%d" % (i, u))
+            nc.vector.tensor_add(out=z[i, u][:], in0=y_ps[i, u][:], in1=bias[:, u * BANK : (u + 1) * BANK])
+
+        def finish(i, u):
+            res = sb.tile([P, BANK], F32, name="res%d_%d" % (i, u))
+            nc.scalar.activation(out=res[:], in_=z[i, u][:], func=SILU)
+            nc.sync.dma_start(out=out[tokens(i), u * BANK : (u + 1) * BANK], in_=res[:])
+
+        wx_op[0] = weight_pass("wx0", wx_raw[0], ("vector", "vector"))
+        wx_op[1] = weight_pass("wx1", wx_raw[1], ("vector", "vector"))
+        interleave_pc(0)
+        interleave_pc(1)
+        round_x("vector", 0, 0)
+        round_x("scalar", 0, 1)
+        x_pass(0, 0)
+        x_pass(0, 1)
+        interleave_pc(2)
+
+        wx_op[2] = operand("wx2", R)
+        lo = round_weight_half("vector", "wx2_bf0", wx_raw[2], 0)
+        hi = round_weight_half("scalar", "wx2_bf1", wx_raw[2], 1)
+        round_x("vector", 0, 2)
+        quantize(wx_op[2], 0, lo, E4M3)
+        quantize_x(0, 2)
+        project_x(0, 2, range(2))
+        quantize(wx_op[2], HALF, hi, E4M3)
+        project_x(0, 2, range(2, 4))
+        interleave_pc(3)
+
+        for g in range(3):
+            round_x("scalar", 1, g)
+        multiply(0)
+        quantize_h(0)
+        project_h(0, 0)
+        project_h(0, 1)
+        x_pass(1, 0)
+        add_bias(0, 0)
+        x_pass(1, 1)
+        x_pass(1, 2)
+        add_bias(0, 1)
+        for g in range(3):
+            round_x("scalar", 2, g)
+        finish(0, 0)
+        multiply(1)
+        x_pass(2, 0)
+        quantize_h(1)
+        project_h(1, 0)
+        x_pass(2, 1)
+        x_pass(2, 2)
+        project_h(1, 1)
+        add_bias(1, 0)
+        for g in range(3):
+            round_x("scalar", 3, g)
+        finish(0, 1)
+        finish(1, 0)
+        multiply(2)
+        x_pass(3, 0)
+        x_pass(3, 1)
+        quantize_h(2)
+        x_pass(3, 2)
+        project_h(2, 0)
+        project_h(2, 1)
+        add_bias(1, 1)
+        finish(1, 1)
+        multiply(3)
+        add_bias(2, 0)
+        finish(2, 0)
+        quantize_h(3)
+        project_h(3, 0)
+        project_h(3, 1)
+        add_bias(2, 1)
+        finish(2, 1)
+        add_bias(3, 0)
+        finish(3, 0)
+        add_bias(3, 1)
+        finish(3, 1)

@@ -55,8 +55,8 @@ def tile_mix_bilin_tm_silu_kernel(tc, x, wx, c, wc, w_words, w_scales, b, out):
             grouped = sb.tile([P, count * PACK], BF16, name=name, align_bytes=64)
             copy_on(
                 engine,
-                grouped[:].rearrange("p (q i j) -> p q j i", i=4, j=PACK),
-                raw[:, :, first : first + count].rearrange("p j (q i) -> p q j i", i=4),
+                grouped[:].rearrange("p (q i j) -> p q j i", i=2, j=PACK),
+                raw[:, :, first : first + count].rearrange("p j (q i) -> p q j i", i=2),
             )
             return grouped
 
@@ -103,20 +103,22 @@ def tile_mix_bilin_tm_silu_kernel(tc, x, wx, c, wc, w_words, w_scales, b, out):
         wc_raw[1] = load_rows("wc_raw1", wc[pass_rows(1), :])
         c_raw[1] = load_rows("c_raw1", c[pass_rows(1), :])
 
-        def load_x(i, g):
-            x_raw[i, g] = load_rows("x_raw%d_%d" % (i, g), x[pass_rows(g), tokens(i)])
+        def load_x(i, g, count):
+            x_raw[i, g] = load_rows("x_raw%d_%d" % (i, g), x[pass_rows(g), i * TOK : (i + count) * TOK])
 
         wx_raw[0] = load_rows("wx_raw0", wx[pass_rows(0), :])
         wx_raw[1] = load_rows("wx_raw1", wx[pass_rows(1), :])
-        load_x(0, 0)
-        load_x(0, 1)
+        load_x(0, 0, 2)
+        load_x(0, 1, 2)
         wx_raw[2] = load_rows("wx_raw2", wx[pass_rows(2), :])
-        load_x(0, 2)
+        load_x(0, 2, 1)
         w_codes = sb.tile([P, 2 * M], U8, name="w_codes", align_bytes=64)
         nc.sync.dma_start(out=w_codes[:].bitcast(I32), in_=w_words[0].bitcast(I32))
-        for i in range(1, tiles):
-            for g in range(x_passes):
-                load_x(i, g)
+        load_x(1, 2, 1)
+        load_x(2, 0, 2)
+        load_x(2, 1, 2)
+        load_x(2, 2, 1)
+        load_x(3, 2, 1)
 
         bias = sb.tile([P, M], F32, name="bias")
         bias_ps = {}
@@ -170,18 +172,21 @@ def tile_mix_bilin_tm_silu_kernel(tc, x, wx, c, wc, w_words, w_scales, b, out):
         def interleave_pc(i):
             pc[i] = sb.tile([P, TOK * PACK], F32, name="pc%d" % i)
             nc.scalar.copy(
-                out=pc[i][:].rearrange("p (t s) -> p t s", s=PACK),
-                in_=pc_rows[:, :, tokens(i)].rearrange("p s t -> p t s"),
+                out=pc[i][:].rearrange("p (q i s) -> p q s i", i=2, s=PACK),
+                in_=pc_rows[:, :, tokens(i)].rearrange("p s (q i) -> p q s i", i=2),
             )
 
         wx_op, x_bf, x_op, px_ps, h_bf, h_op, y_ps, z = {}, {}, {}, {}, {}, {}, {}, {}
 
         def round_x(engine, i, g):
-            x_bf[i, g] = round_columns(engine, "x_bf%d_%d" % (i, g), x_raw[i, g], 0, TOK)
+            x_bf[i, g] = round_columns(engine, "x_bf%d_%d" % (i, g), x_raw[i, g], 0, x_raw[i, g].shape[2])
 
         def quantize_x(i, g):
-            x_op[i, g] = operand("x%d_%d" % (i, g), TOK)
-            quantize(x_op[i, g], 0, x_bf[i, g], E4M3)
+            width = x_raw[i, g].shape[2]
+            op = operand("x%d_%d" % (i, g), width)
+            quantize(op, 0, x_bf[i, g], E4M3)
+            for n in range(width // TOK):
+                x_op[i + n, g] = (op[0][:, tokens(n)], op[1][:, tokens(n)])
 
         def project_x(i, g, slots):
             if i not in px_ps:
@@ -191,8 +196,8 @@ def tile_mix_bilin_tm_silu_kernel(tc, x, wx, c, wc, w_words, w_scales, b, out):
                     out=px_ps[i][:, s * TOK : (s + 1) * TOK],
                     lhsT=wx_op[g][0][:, s * P : (s + 1) * P].bitcast(E4M3),
                     lhsT_scale=wx_op[g][1][:, s * P : (s + 1) * P],
-                    rhs=x_op[i, g][0][:].bitcast(E4M3),
-                    rhs_scale=x_op[i, g][1][:],
+                    rhs=x_op[i, g][0].bitcast(E4M3),
+                    rhs_scale=x_op[i, g][1],
                     start=(g == 0 and s == 0),
                     stop=(g == x_passes - 1 and s == PACK - 1),
                 )
@@ -225,24 +230,32 @@ def tile_mix_bilin_tm_silu_kernel(tc, x, wx, c, wc, w_words, w_scales, b, out):
                 stop=True,
             )
 
-        def add_bias(i, u):
-            z[i, u] = sb.tile([P, BANK], F32, name="z%d_%d" % (i, u))
-            nc.vector.tensor_add(out=z[i, u][:], in0=y_ps[i, u][:], in1=bias[:, u * BANK : (u + 1) * BANK])
+        def add_bias(i, first, count):
+            u = first // BANK
+            z[i, first] = sb.tile([P, count], F32, name="z%d_%d" % (i, first))
+            nc.vector.tensor_add(
+                out=z[i, first][:],
+                in0=y_ps[i, u][:, first - u * BANK : first - u * BANK + count],
+                in1=bias[:, first : first + count],
+            )
 
-        def finish(i, u):
-            res = sb.tile([P, BANK], F32, name="res%d_%d" % (i, u))
-            nc.scalar.activation(out=res[:], in_=z[i, u][:], func=SILU)
-            nc.sync.dma_start(out=out[tokens(i), u * BANK : (u + 1) * BANK], in_=res[:])
+        def finish(i, first):
+            count = z[i, first].shape[1]
+            res = sb.tile([P, count], F32, name="res%d_%d" % (i, first))
+            nc.scalar.activation(out=res[:], in_=z[i, first][:], func=SILU)
+            nc.sync.dma_start(out=out[tokens(i), first : first + count], in_=res[:])
 
+        every = range(PACK)
         wx_op[0] = weight_pass("wx0", wx_raw[0], ("vector", "vector"))
         wx_op[1] = weight_pass("wx1", wx_raw[1], ("vector", "vector"))
-        interleave_pc(0)
-        interleave_pc(1)
+        for i in range(tiles):
+            interleave_pc(i)
         round_x("vector", 0, 0)
         round_x("scalar", 0, 1)
-        x_pass(0, 0)
-        x_pass(0, 1)
-        interleave_pc(2)
+        for g in range(2):
+            quantize_x(0, g)
+            project_x(0, g, every)
+            project_x(1, g, every)
 
         wx_op[2] = operand("wx2", R)
         lo = round_weight_half("vector", "wx2_bf0", wx_raw[2], 0)
@@ -253,52 +266,52 @@ def tile_mix_bilin_tm_silu_kernel(tc, x, wx, c, wc, w_words, w_scales, b, out):
         project_x(0, 2, range(2))
         quantize(wx_op[2], HALF, hi, E4M3)
         project_x(0, 2, range(2, 4))
-        interleave_pc(3)
 
-        for g in range(3):
-            round_x("scalar", 1, g)
+        round_x("scalar", 1, 2)
+        round_x("scalar", 2, 0)
+        round_x("scalar", 2, 1)
+        round_x("scalar", 2, 2)
+        round_x("scalar", 3, 2)
+
         multiply(0)
         quantize_h(0)
         project_h(0, 0)
-        project_h(0, 1)
-        x_pass(1, 0)
-        add_bias(0, 0)
-        x_pass(1, 1)
         x_pass(1, 2)
-        add_bias(0, 1)
-        for g in range(3):
-            round_x("scalar", 2, g)
+        project_h(0, 1)
+        add_bias(0, 0, BANK)
         finish(0, 0)
         multiply(1)
-        x_pass(2, 0)
+        quantize_x(2, 0)
+        project_x(2, 0, every)
         quantize_h(1)
         project_h(1, 0)
+        project_x(3, 0, every)
+        add_bias(0, BANK, BANK)
+        finish(0, BANK)
         x_pass(2, 1)
         x_pass(2, 2)
+        project_x(3, 1, every)
         project_h(1, 1)
-        add_bias(1, 0)
-        for g in range(3):
-            round_x("scalar", 3, g)
-        finish(0, 1)
+        add_bias(1, 0, BANK)
         finish(1, 0)
         multiply(2)
-        x_pass(3, 0)
-        x_pass(3, 1)
-        quantize_h(2)
         x_pass(3, 2)
+        quantize_h(2)
         project_h(2, 0)
         project_h(2, 1)
-        add_bias(1, 1)
-        finish(1, 1)
+        add_bias(1, BANK, BANK)
+        finish(1, BANK)
         multiply(3)
-        add_bias(2, 0)
+        add_bias(2, 0, BANK)
         finish(2, 0)
         quantize_h(3)
         project_h(3, 0)
         project_h(3, 1)
-        add_bias(2, 1)
-        finish(2, 1)
-        add_bias(3, 0)
+        add_bias(2, BANK, BANK)
+        finish(2, BANK)
+        add_bias(3, 0, BANK)
         finish(3, 0)
-        add_bias(3, 1)
-        finish(3, 1)
+        add_bias(3, BANK, HALF)
+        finish(3, BANK)
+        add_bias(3, BANK + HALF, HALF)
+        finish(3, BANK + HALF)

@@ -51,13 +51,16 @@ def tile_mix_bilin_tm_silu_kernel(tc, x, wx, c, wc, w_words, w_scales, b, out):
             scales = sb.tile([P, width], U8, name=name + "_scales", align_bytes=64)
             return codes, scales
 
-        def round_columns(engine, name, raw, first, count):
-            grouped = sb.tile([P, count * PACK], BF16, name=name, align_bytes=64)
+        def round_into(engine, grouped, raw):
             copy_on(
                 engine,
-                grouped[:].rearrange("p (q i j) -> p q j i", i=2, j=PACK),
-                raw[:, :, first : first + count].rearrange("p j (q i) -> p q j i", i=2),
+                grouped.rearrange("p (q i j) -> p q j i", i=2, j=PACK),
+                raw.rearrange("p j (q i) -> p q j i", i=2),
             )
+
+        def round_columns(engine, name, raw, first, count):
+            grouped = sb.tile([P, count * PACK], BF16, name=name, align_bytes=64)
+            round_into(engine, grouped[:], raw[:, :, first : first + count])
             return grouped
 
         def round_weight_half(engine, name, raw, half):
@@ -94,31 +97,36 @@ def tile_mix_bilin_tm_silu_kernel(tc, x, wx, c, wc, w_words, w_scales, b, out):
         wc_raw[0] = load_rows("wc_raw0", wc[pass_rows(0), :])
         b_cols = sb.tile([P, M // P], F32, name="b_cols")
         nc.sync.dma_start(out=b_cols[:], in_=b.rearrange("(n m) -> n m", n=P))
-        for q in range(4):
-            nc.sync.dma_start(
-                out=w_plane[32 * q : 32 * q + 4, :].bitcast(I32),
-                in_=w_scales[0, 4 * q : 4 * q + 4, :].bitcast(I32),
-            )
-        c_raw[0] = load_rows("c_raw0", c[pass_rows(0), :])
         wc_raw[1] = load_rows("wc_raw1", wc[pass_rows(1), :])
+        c_raw[0] = load_rows("c_raw0", c[pass_rows(0), :])
         c_raw[1] = load_rows("c_raw1", c[pass_rows(1), :])
 
         def load_x(i, g, count):
-            x_raw[i, g] = load_rows("x_raw%d_%d" % (i, g), x[pass_rows(g), i * TOK : (i + count) * TOK])
+            raw = load_rows("x_raw%d_%d" % (i, g), x[pass_rows(g), i * TOK : (i + count) * TOK])
+            for n in range(count):
+                x_raw[i + n, g] = (raw, n)
 
-        wx_raw[0] = load_rows("wx_raw0", wx[pass_rows(0), :])
-        wx_raw[1] = load_rows("wx_raw1", wx[pass_rows(1), :])
-        load_x(0, 0, 2)
-        load_x(0, 1, 2)
-        wx_raw[2] = load_rows("wx_raw2", wx[pass_rows(2), :])
-        load_x(0, 2, 1)
         w_codes = sb.tile([P, 2 * M], U8, name="w_codes", align_bytes=64)
-        nc.sync.dma_start(out=w_codes[:].bitcast(I32), in_=w_words[0].bitcast(I32))
-        load_x(1, 2, 1)
-        load_x(2, 0, 2)
-        load_x(2, 1, 2)
-        load_x(2, 2, 1)
-        load_x(3, 2, 1)
+
+        def load_wx(g):
+            wx_raw[g] = load_rows("wx_raw%d" % g, wx[pass_rows(g), :])
+
+        def load_w():
+            nc.sync.dma_start(out=w_codes[:].bitcast(I32), in_=w_words[0].bitcast(I32))
+
+        load_wx(1)
+        load_wx(2)
+        load_x(0, 0, 4)
+        load_wx(0)
+        load_x(0, 1, 4)
+        load_x(0, 2, 2)
+        for r in range(4):
+            nc.sync.dma_start(
+                out=w_plane[r:P:32, :].bitcast(I32),
+                in_=w_scales[0, r:16:4, :].bitcast(I32),
+            )
+        load_w()
+        load_x(2, 2, 2)
 
         bias = sb.tile([P, M], F32, name="bias")
         bias_ps = {}
@@ -140,14 +148,14 @@ def tile_mix_bilin_tm_silu_kernel(tc, x, wx, c, wc, w_words, w_scales, b, out):
             return op
 
         pc_ps = [ps.tile([P, BANK], F32, name="pc_ps%d" % s, tag="acc%d" % s) for s in range(PACK)]
+        wc_op = {}
         for g in range(c_passes):
-            wc_op = weight_pass("wc%d" % g, wc_raw[g], ("vector", "scalar"))
-            if g == 0:
-                for u in range(2):
-                    nc.scalar.copy(
-                        out=bias[:].rearrange("p (n m) -> p n m", m=M // P)[:, :, 4 * u : 4 * u + 4],
-                        in_=bias_ps[u][:].rearrange("p (m n) -> p n m", m=4),
-                    )
+            wc_op[g] = weight_pass("wc%d" % g, wc_raw[g], ("vector", "scalar"))
+            nc.scalar.copy(
+                out=bias[:].rearrange("p (n m) -> p n m", m=M // P)[:, :, 4 * g : 4 * g + 4],
+                in_=bias_ps[g][:].rearrange("p (m n) -> p n m", m=4),
+            )
+        for g in range(c_passes):
             c_op = operand("c%d" % g, T)
             c_lo = round_columns("vector", "c_bf%d_0" % g, c_raw[g], 0, HALF)
             c_hi = round_columns("scalar", "c_bf%d_1" % g, c_raw[g], HALF, HALF)
@@ -156,8 +164,8 @@ def tile_mix_bilin_tm_silu_kernel(tc, x, wx, c, wc, w_words, w_scales, b, out):
             for s in range(PACK):
                 nc.tensor.matmul_mx(
                     out=pc_ps[s][:],
-                    lhsT=wc_op[0][:, s * P : (s + 1) * P].bitcast(E4M3),
-                    lhsT_scale=wc_op[1][:, s * P : (s + 1) * P],
+                    lhsT=wc_op[g][0][:, s * P : (s + 1) * P].bitcast(E4M3),
+                    lhsT_scale=wc_op[g][1][:, s * P : (s + 1) * P],
                     rhs=c_op[0][:].bitcast(E5M2),
                     rhs_scale=c_op[1][:],
                     start=(g == 0),
@@ -178,11 +186,12 @@ def tile_mix_bilin_tm_silu_kernel(tc, x, wx, c, wc, w_words, w_scales, b, out):
 
         wx_op, x_bf, x_op, px_ps, h_bf, h_op, y_ps, z = {}, {}, {}, {}, {}, {}, {}, {}
 
-        def round_x(engine, i, g):
-            x_bf[i, g] = round_columns(engine, "x_bf%d_%d" % (i, g), x_raw[i, g], 0, x_raw[i, g].shape[2])
+        def round_x(engine, i, g, count):
+            raw, n = x_raw[i, g]
+            x_bf[i, g] = round_columns(engine, "x_bf%d_%d" % (i, g), raw, n * TOK, count * TOK)
 
         def quantize_x(i, g):
-            width = x_raw[i, g].shape[2]
+            width = x_bf[i, g].shape[1] // PACK
             op = operand("x%d_%d" % (i, g), width)
             quantize(op, 0, x_bf[i, g], E4M3)
             for n in range(width // TOK):
@@ -204,7 +213,8 @@ def tile_mix_bilin_tm_silu_kernel(tc, x, wx, c, wc, w_words, w_scales, b, out):
 
         def x_pass(i, g):
             quantize_x(i, g)
-            project_x(i, g, range(PACK))
+            for n in range(x_bf[i, g].shape[1] // (PACK * TOK)):
+                project_x(i + n, g, range(PACK))
 
         def multiply(i):
             h_bf[i] = sb.tile([P, TOK * PACK], BF16, name="h_bf%d" % i, align_bytes=64)
@@ -239,79 +249,72 @@ def tile_mix_bilin_tm_silu_kernel(tc, x, wx, c, wc, w_words, w_scales, b, out):
                 in1=bias[:, first : first + count],
             )
 
-        def finish(i, first):
-            count = z[i, first].shape[1]
-            res = sb.tile([P, count], F32, name="res%d_%d" % (i, first))
-            nc.scalar.activation(out=res[:], in_=z[i, first][:], func=SILU)
-            nc.sync.dma_start(out=out[tokens(i), first : first + count], in_=res[:])
+        def finish(i, firsts, queue):
+            start = firsts[0]
+            count = sum(z[i, first].shape[1] for first in firsts)
+            res = sb.tile([P, count], F32, name="res%d_%d" % (i, start))
+            for first in firsts:
+                width = z[i, first].shape[1]
+                nc.scalar.activation(out=res[:, first - start : first - start + width], in_=z[i, first][:], func=SILU)
+            queue.dma_start(out=out[tokens(i), start : start + count], in_=res[:])
 
         every = range(PACK)
-        wx_op[0] = weight_pass("wx0", wx_raw[0], ("vector", "vector"))
         wx_op[1] = weight_pass("wx1", wx_raw[1], ("vector", "vector"))
-        for i in range(tiles):
-            interleave_pc(i)
-        round_x("vector", 0, 0)
-        round_x("scalar", 0, 1)
-        for g in range(2):
-            quantize_x(0, g)
-            project_x(0, g, every)
-            project_x(1, g, every)
-
-        wx_op[2] = operand("wx2", R)
-        lo = round_weight_half("vector", "wx2_bf0", wx_raw[2], 0)
-        hi = round_weight_half("scalar", "wx2_bf1", wx_raw[2], 1)
-        round_x("vector", 0, 2)
-        quantize(wx_op[2], 0, lo, E4M3)
-        quantize_x(0, 2)
-        project_x(0, 2, range(2))
-        quantize(wx_op[2], HALF, hi, E4M3)
-        project_x(0, 2, range(2, 4))
-
-        round_x("scalar", 1, 2)
-        round_x("scalar", 2, 0)
-        round_x("scalar", 2, 1)
-        round_x("scalar", 2, 2)
-        round_x("scalar", 3, 2)
-
+        wx_op[2] = weight_pass("wx2", wx_raw[2], ("vector", "vector"))
+        interleave_pc(0)
+        interleave_pc(1)
+        interleave_pc(2)
+        interleave_pc(3)
+        round_x("vector", 0, 0, 4)
+        quantize_x(0, 0)
+        wx_op[0] = weight_pass("wx0", wx_raw[0], ("vector", "scalar"))
+        project_x(0, 0, every)
+        project_x(1, 0, every)
+        project_x(2, 0, every)
+        project_x(3, 0, every)
+        round_x("vector", 0, 1, 2)
+        round_x("scalar", 2, 1, 2)
+        x_pass(0, 1)
+        round_x("vector", 0, 2, 1)
+        round_x("scalar", 1, 2, 1)
+        x_pass(0, 2)
+        x_pass(1, 2)
+        x_pass(2, 1)
+        round_x("scalar", 2, 2, 1)
+        round_x("scalar", 3, 2, 1)
         multiply(0)
+        multiply(1)
         quantize_h(0)
         project_h(0, 0)
-        x_pass(1, 2)
         project_h(0, 1)
-        add_bias(0, 0, BANK)
-        finish(0, 0)
-        multiply(1)
-        quantize_x(2, 0)
-        project_x(2, 0, every)
         quantize_h(1)
         project_h(1, 0)
-        project_x(3, 0, every)
-        add_bias(0, BANK, BANK)
-        finish(0, BANK)
-        x_pass(2, 1)
-        x_pass(2, 2)
-        project_x(3, 1, every)
         project_h(1, 1)
-        add_bias(1, 0, BANK)
-        finish(1, 0)
-        multiply(2)
+        x_pass(2, 2)
+        add_bias(0, 0, BANK)
+        finish(0, [0], nc.sync)
         x_pass(3, 2)
+        add_bias(0, BANK, BANK)
+        finish(0, [BANK], nc.sync)
+        multiply(2)
+        add_bias(1, 0, BANK)
+        finish(1, [0], nc.sync)
         quantize_h(2)
         project_h(2, 0)
         project_h(2, 1)
-        add_bias(1, BANK, BANK)
-        finish(1, BANK)
         multiply(3)
-        add_bias(2, 0, BANK)
-        finish(2, 0)
+        add_bias(1, BANK, BANK)
+        finish(1, [BANK], nc.sync)
         quantize_h(3)
         project_h(3, 0)
         project_h(3, 1)
+        add_bias(2, 0, BANK)
+        finish(2, [0], nc.sync)
         add_bias(2, BANK, BANK)
-        finish(2, BANK)
-        add_bias(3, 0, BANK)
-        finish(3, 0)
+        finish(2, [BANK], nc.sync)
+        add_bias(3, 0, HALF)
+        add_bias(3, HALF, HALF)
+        finish(3, [0, HALF], nc.sync)
         add_bias(3, BANK, HALF)
-        finish(3, BANK)
         add_bias(3, BANK + HALF, HALF)
-        finish(3, BANK + HALF)
+        finish(3, [BANK, BANK + HALF], nc.scalar)

from contextlib import ExitStack

import concourse.mybir as mybir
from concourse.masks import make_identity

K, L, R, M, T = 1536, 1024, 512, 1024, 512
FLOPS = 2 * (K * R * T + L * R * T + R * M * T)

F32 = mybir.dt.float32
BF16 = mybir.dt.bfloat16
I32 = mybir.dt.int32
U32 = mybir.dt.uint32
U8 = mybir.dt.uint8
E4M3 = mybir.dt.float8_e4m3fn_x4
E5M2 = mybir.dt.float8_e5m2_x4
E2M1 = mybir.dt.float4_e2m1fn_x4
SILU = mybir.ActivationFunctionType.Silu

P = 128
PACK = 4
K_PASS = P * PACK
BANK = 512
TOK = 128
HALF = 256


def tile_mix_bilin_tm_silu_kernel(tc, x, wx, c, wc, w_words, w_scales, b, out):
    nc = tc.nc
    x_passes = K // K_PASS
    c_passes = L // K_PASS
    tiles = T // TOK

    with ExitStack() as ctx:
        sb = ctx.enter_context(tc.tile_pool(name="sb", bufs=1))
        ps = ctx.enter_context(tc.psum_pool(name="ps", bufs=1))
        ctx.enter_context(tc.manual_schedule())

        def copy_on(engine, dst, src):
            if engine == "vector":
                nc.vector.tensor_copy(out=dst, in_=src)
            else:
                nc.scalar.copy(out=dst, in_=src)

        def load_rows(name, rows):
            raw = sb.tile([P, PACK, rows.shape[1]], F32, name=name)
            nc.sync.dma_start(out=raw[:], in_=rows.rearrange("(p j) w -> p j w", j=PACK))
            return raw

        def operand(name, width):
            codes = sb.tile([P, width], U32, name=name + "_codes", align_bytes=64)
            scales = sb.tile([P, width], U8, name=name + "_scales", align_bytes=64)
            return codes, scales

        def round_into(engine, grouped, raw):
            copy_on(
                engine,
                grouped.rearrange("p (q i j) -> p q j i", i=2, j=PACK),
                raw.rearrange("p j (q i) -> p q j i", i=2),
            )

        def round_columns(engine, name, raw, first, count):
            grouped = sb.tile([P, count * PACK], BF16, name=name, align_bytes=64)
            round_into(engine, grouped[:], raw[:, :, first : first + count])
            return grouped

        def round_weight_half(engine, name, raw, half):
            grouped = sb.tile([P, HALF * PACK], BF16, name=name, align_bytes=64)
            copy_on(
                engine,
                grouped[:].rearrange("p (s m j) -> p m j s", s=2, j=PACK),
                raw[:].rearrange("p j (m s) -> p m j s", s=PACK)[:, :, :, 2 * half : 2 * half + 2],
            )
            return grouped

        def quantize(op, first, grouped, fmt):
            count = grouped.shape[1] // PACK
            nc.vector.quantize_mx(
                out=op[0][:, first : first + count].bitcast(fmt),
                scales=op[1][:, first : first + count],
                in_=grouped[:],
            )

        def pass_rows(g):
            return slice(g * K_PASS, (g + 1) * K_PASS)

        def tokens(i):
            return slice(i * TOK, (i + 1) * TOK)

        w_plane = sb.tile([P, M], U8, name="w_plane", align_bytes=64)
        nc.vector.memset(w_plane[:].bitcast(I32), 0)
        ident = sb.tile([P, P], F32, name="ident")
        make_identity(nc, ident[:])
        warm = sb.tile([P, 1], F32, name="warm")
        nc.scalar.activation(out=warm[:], in_=ident[:, 0:1], func=SILU)

        wc_raw, c_raw, wx_raw, x_raw = {}, {}, {}, {}
        wc_raw[0] = load_rows("wc_raw0", wc[pass_rows(0), :])
        b_cols = sb.tile([P, M // P], F32, name="b_cols")
        nc.sync.dma_start(out=b_cols[:], in_=b.rearrange("(n m) -> n m", n=P))
        wc_raw[1] = load_rows("wc_raw1", wc[pass_rows(1), :])
        c_raw[0] = load_rows("c_raw0", c[pass_rows(0), :])
        c_raw[1] = load_rows("c_raw1", c[pass_rows(1), :])

        def load_x(i, g, count):
            raw = load_rows("x_raw%d_%d" % (i, g), x[pass_rows(g), i * TOK : (i + count) * TOK])
            for n in range(count):
                x_raw[i + n, g] = (raw, n)

        w_codes = sb.tile([P, 2 * M], U8, name="w_codes", align_bytes=64)

        def load_wx(g):
            wx_raw[g] = load_rows("wx_raw%d" % g, wx[pass_rows(g), :])

        def load_w():
            nc.sync.dma_start(out=w_codes[:].bitcast(I32), in_=w_words[0].bitcast(I32))

        load_wx(1)
        load_wx(2)
        load_x(0, 0, 4)
        load_wx(0)
        load_x(0, 1, 4)
        load_x(0, 2, 2)
        for r in range(4):
            nc.sync.dma_start(
                out=w_plane[r:P:32, :].bitcast(I32),
                in_=w_scales[0, r:16:4, :].bitcast(I32),
            )
        load_w()
        load_x(2, 2, 2)

        bias = sb.tile([P, M], F32, name="bias")
        bias_ps = {}
        for u in range(2):
            bias_ps[u] = ps.tile([P, BANK], F32, name="bias_ps%d" % u, tag="px%d" % (2 + u))
            for m in range(4):
                col = 4 * u + m
                nc.tensor.transpose(
                    bias_ps[u][:, m * P : (m + 1) * P],
                    b_cols[:, col : col + 1].to_broadcast([P, P]),
                    ident[:],
                )

        def weight_pass(name, raw, engines):
            op = operand(name, R)
            halves = [round_weight_half(engines[u], "%s_bf%d" % (name, u), raw, u) for u in range(2)]
            for u in range(2):
                quantize(op, u * HALF, halves[u], E4M3)
            return op

        pc_ps = [ps.tile([P, BANK], F32, name="pc_ps%d" % s, tag="acc%d" % s) for s in range(PACK)]
        wc_op = {}
        for g in range(c_passes):
            wc_op[g] = weight_pass("wc%d" % g, wc_raw[g], ("vector", "scalar"))
            nc.scalar.copy(
                out=bias[:].rearrange("p (n m) -> p n m", m=M // P)[:, :, 4 * g : 4 * g + 4],
                in_=bias_ps[g][:].rearrange("p (m n) -> p n m", m=4),
            )
        for g in range(c_passes):
            c_op = operand("c%d" % g, T)
            c_lo = round_columns("vector", "c_bf%d_0" % g, c_raw[g], 0, HALF)
            c_hi = round_columns("scalar", "c_bf%d_1" % g, c_raw[g], HALF, HALF)
            quantize(c_op, 0, c_lo, E5M2)
            quantize(c_op, HALF, c_hi, E5M2)
            for s in range(PACK):
                nc.tensor.matmul_mx(
                    out=pc_ps[s][:],
                    lhsT=wc_op[g][0][:, s * P : (s + 1) * P].bitcast(E4M3),
                    lhsT_scale=wc_op[g][1][:, s * P : (s + 1) * P],
                    rhs=c_op[0][:].bitcast(E5M2),
                    rhs_scale=c_op[1][:],
                    start=(g == 0),
                    stop=(g == c_passes - 1),
                )

        pc_rows = sb.tile([P, PACK, T], F32, name="pc_rows")
        for s in range(PACK):
            nc.scalar.copy(out=pc_rows[:, s, :], in_=pc_ps[s][:])
        pc = {}

        def interleave_pc(i):
            pc[i] = sb.tile([P, TOK * PACK], F32, name="pc%d" % i)
            nc.scalar.copy(
                out=pc[i][:].rearrange("p (q i s) -> p q s i", i=2, s=PACK),
                in_=pc_rows[:, :, tokens(i)].rearrange("p s (q i) -> p q s i", i=2),
            )

        wx_op, x_bf, x_op, px_ps, h_bf, h_op, y_ps, z = {}, {}, {}, {}, {}, {}, {}, {}

        def round_x(engine, i, g, count):
            raw, n = x_raw[i, g]
            x_bf[i, g] = round_columns(engine, "x_bf%d_%d" % (i, g), raw, n * TOK, count * TOK)

        def quantize_x(i, g):
            width = x_bf[i, g].shape[1] // PACK
            op = operand("x%d_%d" % (i, g), width)
            quantize(op, 0, x_bf[i, g], E4M3)
            for n in range(width // TOK):
                x_op[i + n, g] = (op[0][:, tokens(n)], op[1][:, tokens(n)])

        def project_x(i, g, slots):
            if i not in px_ps:
                px_ps[i] = ps.tile([P, BANK], F32, name="px_ps%d" % i, tag="px%d" % i)
            for s in slots:
                nc.tensor.matmul_mx(
                    out=px_ps[i][:, s * TOK : (s + 1) * TOK],
                    lhsT=wx_op[g][0][:, s * P : (s + 1) * P].bitcast(E4M3),
                    lhsT_scale=wx_op[g][1][:, s * P : (s + 1) * P],
                    rhs=x_op[i, g][0].bitcast(E4M3),
                    rhs_scale=x_op[i, g][1],
                    start=(g == 0 and s == 0),
                    stop=(g == x_passes - 1 and s == PACK - 1),
                )

        def x_pass(i, g):
            quantize_x(i, g)
            for n in range(x_bf[i, g].shape[1] // (PACK * TOK)):
                project_x(i + n, g, range(PACK))

        def multiply(i):
            h_bf[i] = sb.tile([P, TOK * PACK], BF16, name="h_bf%d" % i, align_bytes=64)
            nc.vector.tensor_mul(
                out=h_bf[i][:].rearrange("p (t s) -> p t s", s=PACK),
                in0=px_ps[i][:].rearrange("p (s t) -> p t s", s=PACK),
                in1=pc[i][:].rearrange("p (t s) -> p t s", s=PACK),
            )

        def quantize_h(i):
            h_op[i] = operand("h%d" % i, TOK)
            quantize(h_op[i], 0, h_bf[i], E4M3)

        def project_h(i, u):
            y_ps[i, u] = ps.tile([P, BANK], F32, name="y_ps%d_%d" % (i, u), tag="acc%d" % ((2 * i + u) % 4))
            nc.tensor.matmul_mx(
                out=y_ps[i, u][:],
                lhsT=h_op[i][0][:].bitcast(E4M3),
                lhsT_scale=h_op[i][1][:],
                rhs=w_codes[:, 2 * u * BANK : 2 * (u + 1) * BANK].bitcast(E2M1),
                rhs_scale=w_plane[:, u * BANK : (u + 1) * BANK],
                start=True,
                stop=True,
            )

        def add_bias(i, first, count):
            u = first // BANK
            z[i, first] = sb.tile([P, count], F32, name="z%d_%d" % (i, first))
            nc.vector.tensor_add(
                out=z[i, first][:],
                in0=y_ps[i, u][:, first - u * BANK : first - u * BANK + count],
                in1=bias[:, first : first + count],
            )

        def finish(i, firsts, queue):
            start = firsts[0]
            count = sum(z[i, first].shape[1] for first in firsts)
            res = sb.tile([P, count], F32, name="res%d_%d" % (i, start))
            for first in firsts:
                width = z[i, first].shape[1]
                nc.scalar.activation(out=res[:, first - start : first - start + width], in_=z[i, first][:], func=SILU)
            queue.dma_start(out=out[tokens(i), start : start + count], in_=res[:])

        every = range(PACK)
        wx_op[1] = weight_pass("wx1", wx_raw[1], ("vector", "vector"))
        wx_op[2] = weight_pass("wx2", wx_raw[2], ("vector", "vector"))
        interleave_pc(0)
        interleave_pc(1)
        interleave_pc(2)
        interleave_pc(3)
        round_x("vector", 0, 0, 4)
        quantize_x(0, 0)
        wx_op[0] = weight_pass("wx0", wx_raw[0], ("vector", "scalar"))
        project_x(0, 0, every)
        project_x(1, 0, every)
        project_x(2, 0, every)
        project_x(3, 0, every)
        round_x("vector", 0, 1, 2)
        round_x("scalar", 2, 1, 2)
        x_pass(0, 1)
        round_x("vector", 0, 2, 1)
        round_x("scalar", 1, 2, 1)
        x_pass(0, 2)
        x_pass(1, 2)
        x_pass(2, 1)
        round_x("scalar", 2, 2, 1)
        round_x("scalar", 3, 2, 1)
        multiply(0)
        multiply(1)
        quantize_h(0)
        project_h(0, 0)
        project_h(0, 1)
        quantize_h(1)
        project_h(1, 0)
        project_h(1, 1)
        x_pass(2, 2)
        add_bias(0, 0, BANK)
        finish(0, [0], nc.sync)
        x_pass(3, 2)
        add_bias(0, BANK, BANK)
        finish(0, [BANK], nc.sync)
        multiply(2)
        add_bias(1, 0, BANK)
        finish(1, [0], nc.sync)
        quantize_h(2)
        project_h(2, 0)
        project_h(2, 1)
        multiply(3)
        add_bias(1, BANK, BANK)
        finish(1, [BANK], nc.sync)
        quantize_h(3)
        project_h(3, 0)
        project_h(3, 1)
        add_bias(2, 0, BANK)
        finish(2, [0], nc.sync)
        add_bias(2, BANK, BANK)
        finish(2, [BANK], nc.sync)
        add_bias(3, 0, HALF)
        add_bias(3, HALF, HALF)
        finish(3, [0, HALF], nc.sync)
        add_bias(3, BANK, HALF)
        add_bias(3, BANK + HALF, HALF)
        finish(3, [BANK, BANK + HALF], nc.scalar)
